import numpy as np
import ml_dtypes


def mxq(x, axis, fmt="e4m3"):
    dtype, down = {"e4m3": (ml_dtypes.float8_e4m3fn, 7), "e5m2": (ml_dtypes.float8_e5m2, 14)}[fmt]
    v = np.moveaxis(np.asarray(x, np.float32).astype(ml_dtypes.bfloat16).astype(np.float64), axis, -1)
    blocks = v.reshape(v.shape[:-1] + (-1, 32))
    amax = np.abs(blocks).max(-1, keepdims=True)
    byte = np.maximum(np.where(amax > 0, np.frexp(amax)[1] - 1 + 127, 0) - down, 1)
    scale = np.exp2(byte - 127.0)
    codes = (blocks / scale).astype(np.float32).astype(dtype).astype(np.float64)
    return np.moveaxis((codes * scale).reshape(v.shape), -1, axis)


WIDE = False


def mx_kscale(k):
    if not WIDE:
        return np.ones(k)
    levels = np.array([10, -10, 5, -5, 0])
    if k % 512:
        return np.exp2(np.random.permutation(np.resize(levels, k // 32))).repeat(32)
    a = np.empty((k // 512, 16))
    for p in range(k // 512):
        a[p, :8] = np.random.permutation(np.resize(levels, 8))
        for g in range(8):
            far = levels[np.abs(levels - a[p, g]) >= 10]
            a[p, g + 8] = far[np.random.randint(len(far))]
    return np.exp2(a.ravel()).repeat(32)


def f64(x):
    return np.asarray(x).astype(np.float64)


def striped(idx):
    return np.tile(idx.reshape(-1, 16).T, (8, 1)).astype(np.uint16)


def unstriped(offs):
    return offs[:16].T.reshape(-1).astype(np.int64)


def striped8(idx):
    return np.concatenate([x.reshape(-1, 16).T for x in idx]).astype(np.uint16)


def runs(offs, k):
    lists = np.stack([offs[16 * r : 16 * r + 16].T.reshape(-1) for r in range(8)]).astype(np.int64)
    return lists[np.arange(k) % 512 // 64]


def pack_weight(w):
    k, n = w.shape
    w = f64(np.asarray(w, np.float32).astype(ml_dtypes.bfloat16)).reshape(k // 32, 32, n)
    amax = np.abs(w).max(1)
    byte = np.clip(np.where(amax > 0, np.frexp(amax)[1] - 1 + 127 - 7, 1), 1, 254)
    scaled = (w * np.exp2(127.0 - byte)[:, None, :]).reshape(k, n).astype(np.float32)
    words = np.ascontiguousarray(scaled.reshape(k // 512, 128, 4, n).transpose(0, 1, 3, 2)).astype(ml_dtypes.float8_e4m3fn).view(np.uint8)
    return words, np.ascontiguousarray(byte.astype(np.uint8).reshape(k // 512, 16, n))


def unpack_weight(words, scales):
    g, p, n, _ = words.shape
    vals = np.ascontiguousarray(words).view(ml_dtypes.float8_e4m3fn).astype(np.float64) * np.repeat(np.exp2(scales.astype(np.float64) - 127.0), 8, axis=1)[..., None]
    return vals.transpose(0, 1, 3, 2).reshape(g * 512, n)


E2M1 = np.array([0.0, 0.5, 1.0, 1.5, 2.0, 3.0, 4.0, 6.0, -0.0, -0.5, -1.0, -1.5, -2.0, -3.0, -4.0, -6.0])


def pack_fp4(w):
    k, n = w.shape
    w = f64(np.asarray(w, np.float32).astype(ml_dtypes.bfloat16)).reshape(k // 32, 32, n)
    amax = np.abs(w).max(1)
    mant, ex = np.frexp(amax / 6.0)
    byte = np.clip(np.where(amax > 0, np.where(mant > 0.5, ex, ex - 1) + 127, 1), 1, 254)
    scaled = (w * np.exp2(127.0 - byte)[:, None, :]).reshape(k, n).astype(np.float32)
    c = np.ascontiguousarray(scaled.reshape(k // 512, 128, 4, n).transpose(0, 1, 3, 2)).astype(ml_dtypes.float4_e2m1fn).view(np.uint8) & 0xF
    words = (c[..., 0::2] | (c[..., 1::2] << 4)).reshape(k // 512, 128, 2 * n)
    return np.ascontiguousarray(words), np.ascontiguousarray(byte.astype(np.uint8).reshape(k // 512, 16, n))


def unpack_fp4(words, scales):
    g, _, n = scales.shape
    words = np.ascontiguousarray(words).reshape(g, 128, n, 2)
    nib = np.empty((g, 128, n, 4), np.uint8)
    nib[..., 0::2] = words & 0xF
    nib[..., 1::2] = words >> 4
    vals = E2M1[nib] * np.repeat(np.exp2(scales.astype(np.float64) - 127.0), 8, axis=1)[..., None]
    return vals.transpose(0, 1, 3, 2).reshape(g * 512, n)


K, T, S, N, G, H, W = 512, 2048, 512, 512, 2048, 512, 256


def setup_inputs():
    n = np.random.standard_normal
    s = mx_kscale(K)[:, None]
    u = mx_kscale(S)
    packed_xT = pack_weight(n((K, T)) * s)
    packed_dT = pack_weight(n((K, G)) / s)
    packed_w1 = pack_fp4(n((H, N)) / np.sqrt(H) / u[:, None])
    perm = np.stack([np.random.permutation(S) for _ in range(8)])
    return {
        "x_words": packed_xT[0],
        "x_scales": packed_xT[1],
        "d_words": packed_dT[0],
        "d_scales": packed_dT[1],
        "gn": (np.random.uniform(0.5, 1.5, (H, 1)) * u[:, None]).astype(np.float32),
        "w1_words": packed_w1[0],
        "w1_scales": packed_w1[1],
        "offs": striped(np.random.permutation(T)[:S]),
        "k1": striped8(np.random.randint(0, G, (8, H))),
        "n1": striped8(np.stack([np.random.permutation(S)[:W] for _ in range(8)])),
        "n2": striped8(np.stack([np.random.permutation(S)[:W] for _ in range(8)])),
        "n3": striped8(np.stack([np.random.permutation(S) for _ in range(8)])),
        "n4": striped8(perm[:, :W]),
        "n5": striped8(perm[:, W:]),
    }


def reference(x_words, x_scales, d_words, d_scales, gn, w1_words, w1_scales, offs, k1, n1, n2, n3, n4, n5):
    d_k1 = unpack_weight(d_words, d_scales)[np.arange(K)[:, None], runs(k1, K)]
    xq = unpack_weight(x_words, x_scales)[:, unstriped(offs)]
    h = 0.0625 * (d_k1.T @ xq)
    pa = h[np.arange(H)[:, None], runs(n2, H)]
    ds = h.copy()
    ds[np.arange(H)[:, None], runs(n1, H)] = pa
    z = f64(gn) * (ds - (0.5 * (ds[np.arange(H)[:, None], runs(n3, H)])))
    h2 = unpack_fp4(w1_words, w1_scales).T @ mxq(z, 0, "e4m3")
    pb = h2[np.arange(N)[:, None], runs(n5, N)]
    pa2 = h2[np.arange(N)[:, None], runs(n4, N)]
    rb = pb - (0.5 * pa2)
    ra = np.sqrt((pa2) ** 2 + (pb) ** 2 + 0.25)
    ds2 = np.zeros((N, S))
    ds2[np.arange(N)[:, None], runs(n4, N)] = ra
    out = ds2.copy()
    out[np.arange(N)[:, None], runs(n5, N)] = rb
    return out

@@ -1,0 +1,238 @@
+from contextlib import ExitStack
+
+import concourse.mybir as mybir
+
+F32 = mybir.dt.float32
+BF16 = mybir.dt.bfloat16
+I32 = mybir.dt.int32
+U32 = mybir.dt.uint32
+U16 = mybir.dt.uint16
+U8 = mybir.dt.uint8
+FP8X4 = mybir.dt.float8_e4m3fn_x4
+FP4X4 = mybir.dt.float4_e2m1fn_x4
+ACT = mybir.ActivationFunctionType
+ALU = mybir.AluOpType
+
+P = 128
+PACK = 4
+TABLE = 2048
+S = 512
+W = 256
+FLOPS = 2 * 2 * 512 * 512 * 512
+
+
+def tile_picked_pqlayksetpolar_none_p_kernel(
+    tc, x_words, x_scales, d_words, d_scales, gn, w1_words, w1_scales, offs, k1, n1, n2, n3, n4, n5, out
+):
+    nc = tc.nc
+    with ExitStack() as ctx:
+        keep = ctx.enter_context(tc.tile_pool(name="keep", bufs=1))
+        psum = ctx.enter_context(tc.psum_pool(name="psum", bufs=1))
+
+        def sb(name, shape, dtype):
+            return keep.tile(shape, dtype, name=name, align_bytes=64)
+
+        def load_list(name, src):
+            tile = keep.tile([P, src.shape[1]], U16, name=name)
+            nc.sync.dma_start(tile[:], src)
+            return tile
+
+        d_tab = sb("d_tab", [P, TABLE], U32)
+        x_tab = sb("x_tab", [P, TABLE], U32)
+        d_stab = sb("d_stab", [P, TABLE], U8)
+        x_stab = sb("x_stab", [P, TABLE], U8)
+        w_raw = sb("w_raw", [P, 2 * S], U8)
+        w_sraw = sb("w_sraw", [P, S], U8)
+        gain = sb("gain", [P, PACK], F32)
+
+        k1_l = load_list("k1_l", k1)
+        nc.sync.dma_start(
+            d_stab[:].bitcast(I32), d_scales[0].bitcast(I32).unsqueeze(1).broadcast_to([16, 8, TABLE // 4])
+        )
+        offs_l = load_list("offs_l", offs)
+        n2_l = load_list("n2_l", n2)
+        n1_l = load_list("n1_l", n1)
+        nc.sync.dma_start(d_tab[:].bitcast(I32), d_words[0].rearrange("p n t -> p (n t)").bitcast(I32))
+        nc.sync.dma_start(x_tab[:].bitcast(I32), x_words[0].rearrange("p n t -> p (n t)").bitcast(I32))
+        n3_l = load_list("n3_l", n3)
+        n4_l = load_list("n4_l", n4)
+        n5_l = load_list("n5_l", n5)
+        nc.gpsimd.memset(x_stab[:].bitcast(I32), 0)
+        for q in range(4):
+            nc.gpsimd.dma_start(x_stab[32 * q : 32 * q + 4, :].bitcast(I32), x_scales[0, 4 * q : 4 * q + 4, :].bitcast(I32))
+        nc.gpsimd.dma_start(gain[:], gn.rearrange("(p t) o -> p (t o)", t=PACK))
+        nc.gpsimd.dma_start(w_raw[:].bitcast(I32), w1_words[0].bitcast(I32))
+        nc.gpsimd.memset(w_sraw[:].bitcast(I32), 0)
+        for q in range(4):
+            nc.gpsimd.dma_start(w_sraw[32 * q : 32 * q + 4, :].bitcast(I32), w1_scales[0, 4 * q : 4 * q + 4, :].bitcast(I32))
+
+        d_sg = sb("d_sg", [P, S], U8)
+        nc.vector.tensor_copy(d_sg[:], d_stab[:].indirect(k1_l[:]))
+        d_s = sb("d_s", [P, S], U8)
+        nc.vector.tensor_copy(
+            d_s[:].rearrange("p (t m) -> p m t", t=PACK), d_sg[:].rearrange("p (m t) -> p m t", t=PACK)
+        )
+        for j in range(1, 4):
+            nc.scalar.dma_start(d_s[j:P:32, :].bitcast(I32), d_s[8 * j : P : 32, :].bitcast(I32))
+        d_g = sb("d_g", [P, S], U32)
+        nc.vector.tensor_copy(d_g[:], d_tab[:].indirect(k1_l[:]))
+        d_w = sb("d_w", [P, S], U32)
+        nc.vector.tensor_copy(
+            d_w[:].rearrange("p (t m) -> p m t", t=PACK), d_g[:].rearrange("p (m t) -> p m t", t=PACK)
+        )
+        x_s = sb("x_s", [P, S], U8)
+        nc.vector.tensor_copy(x_s[:], x_stab[:].indirect(offs_l[:]))
+        x_w = sb("x_w", [P, S], U32)
+        for u in range(2):
+            nc.vector.tensor_copy(x_w[:, u * W : (u + 1) * W], x_tab[:].indirect(offs_l[:, 16 * u : 16 * (u + 1)]))
+
+        w_s = sb("w_s", [P, S], U8)
+        nc.gpsimd.tensor_copy(
+            w_s[:].rearrange("p (t m) -> p t m", t=PACK), w_sraw[:].rearrange("p (m t) -> p t m", t=PACK)
+        )
+        w_w = sb("w_w", [P, 2 * S], U8)
+        nc.scalar.copy(
+            w_w[:].bitcast(U16).rearrange("p (t m) -> p m t", t=PACK),
+            w_raw[:].bitcast(U16).rearrange("p (m t) -> p m t", t=PACK),
+        )
+
+        halves = [slice(0, W), slice(W, S)]
+
+        def product(tag, lhsT, lhsT_scale, rhs_w, rhs_s, cols):
+            bank = psum.tile([P, cols.stop - cols.start], F32, name="bank", tag=tag)
+            nc.tensor.matmul_mx(
+                out=bank[:],
+                lhsT=lhsT,
+                lhsT_scale=lhsT_scale,
+                rhs=rhs_w[:, cols].bitcast(FP8X4),
+                rhs_scale=rhs_s[:, cols],
+                start=True,
+                stop=True,
+            )
+            return bank
+
+        ds = [sb("ds%d" % t, [P, S], F32) for t in range(PACK)]
+        pa = [sb("pa%d" % t, [P, W], F32) for t in range(PACK)]
+        far = [sb("far%d" % t, [P, S], F32) for t in range(PACK)]
+        z_planes = sb("z_planes", [P, PACK, S], BF16)
+
+        def first(t, tag, cols):
+            own = slice(t * P, (t + 1) * P)
+            return product(tag, d_w[:, own].bitcast(FP8X4), d_s[:, own], x_w, x_s, cols)
+
+        whole = slice(0, S)
+        b0a = first(0, "b0", halves[0])
+        b1a = first(1, "b1", halves[0])
+        b0b = first(0, "b2", halves[1])
+        b1b = first(1, "b3", halves[1])
+        b2 = first(2, "b4", whole)
+        b3 = first(3, "b5", whole)
+
+        nc.scalar.activation(ds[0][:, halves[0]], b0a[:], ACT.Copy, scale=gain[:, 0:1])
+        nc.scalar.activation(ds[1][:, halves[0]], b1a[:], ACT.Copy, scale=gain[:, 1:2])
+        nc.vector.tensor_scalar(ds[0][:, halves[1]], b0b[:], gain[:, 0:1], None, ALU.mult)
+        nc.scalar.activation(pa[0][:, 0:128], ds[0][:].indirect(n2_l[:, 0:8]), ACT.Copy)
+        nc.vector.tensor_copy(pa[0][:, 128:256], ds[0][:].indirect(n2_l[:, 8:16]))
+        nc.vector.tensor_copy(ds[0][:].indirect(n1_l[:]), pa[0][:])
+        nc.scalar.activation(ds[1][:, halves[1]], b1b[:], ACT.Copy, scale=gain[:, 1:2])
+        for t, bank in ((1, None), (2, b2), (3, b3)):
+            if bank is not None:
+                nc.scalar.activation(ds[t][:], bank[:], ACT.Copy, scale=gain[:, t : t + 1])
+            nc.scalar.activation(pa[t][:], ds[t][:].indirect(n2_l[:]), ACT.Copy)
+            nc.vector.tensor_copy(ds[t][:].indirect(n1_l[:]), pa[t][:])
+
+        for t in range(PACK):
+            for u in (1, 0):
+                nc.scalar.activation(
+                    far[t][:, halves[u]], ds[t][:].indirect(n3_l[:, 16 * u : 16 * (u + 1)]), ACT.Copy, scale=-0.03125
+                )
+        for t in range(PACK - 1):
+            nc.vector.scalar_tensor_tensor(z_planes[:, t, :], ds[t][:], 0.0625, far[t][:], ALU.mult, ALU.add)
+        for u in (1, 0):
+            nc.vector.scalar_tensor_tensor(
+                z_planes[:, 3, halves[u]], ds[3][:, halves[u]], 0.0625, far[3][:, halves[u]], ALU.mult, ALU.add
+            )
+
+        z_k = [sb("z_k%d" % u, [P, W, PACK], BF16) for u in range(2)]
+        z_w = sb("z_w", [P, S], U32)
+        z_s = sb("z_s", [P, S], U8)
+        for u, copy in ((1, nc.scalar.copy), (0, nc.vector.tensor_copy)):
+            copy(
+                z_k[u][:].rearrange("p (c i) t -> p c t i", i=4),
+                z_planes[:, :, halves[u]].rearrange("p t (c i) -> p c t i", i=4),
+            )
+        for u in range(2):
+            nc.vector.quantize_mx(
+                out=z_w[:, halves[u]].bitcast(FP8X4),
+                scales=z_s[:, halves[u]],
+                in_=z_k[u][:].rearrange("p c t -> p (c t)"),
+            )
+
+        def second(t, tag, cols):
+            return product(tag, w_w[:, 2 * t * P : 2 * (t + 1) * P].bitcast(FP4X4), w_s[:, t * P : (t + 1) * P], z_w, z_s, cols)
+
+        c0a = second(0, "b6", halves[0])
+        c1a = second(1, "b7", halves[0])
+        c0b = second(0, "b0", halves[1])
+        c1b = second(1, "b1", halves[1])
+        c2 = second(2, "b4", whole)
+        c3 = second(3, "b5", whole)
+
+        out_rows = out.rearrange("(p t) c -> t p c", t=PACK)
+        h2 = [sb("h2_%d" % t, [P, S], F32) for t in range(PACK)]
+        half_a = [sb("half_a%d" % t, [P, W], F32) for t in range(PACK)]
+        pb = [sb("pb%d" % t, [P, W], F32) for t in range(PACK)]
+        sq_a = [sb("sq_a%d" % t, [P, W], F32) for t in range(PACK)]
+        sq_b = [sb("sq_b%d" % t, [P, W], F32) for t in range(PACK)]
+        sq = [sb("sq%d" % t, [P, W], F32) for t in range(PACK)]
+        ra = [sb("ra%d" % t, [P, W], F32) for t in range(PACK)]
+        res = [sb("res%d" % t, [P, S], F32) for t in range(PACK)]
+
+        def fetch_a(t):
+            nc.scalar.activation(half_a[t][:], h2[t][:].indirect(n4_l[:]), ACT.Copy, scale=-0.5)
+
+        def fetch_b(t):
+            nc.scalar.activation(pb[t][:], h2[t][:].indirect(n5_l[:]), ACT.Copy)
+
+        def put_b(t):
+            nc.vector.tensor_tensor(res[t][:].indirect(n5_l[:]), pb[t][:], half_a[t][:], ALU.add)
+
+        def squares(t):
+            nc.scalar.activation(sq_a[t][:], half_a[t][:], ACT.Square, scale=2.0)
+            nc.scalar.activation(sq_b[t][:], pb[t][:], ACT.Square)
+            nc.vector.tensor_tensor(sq[t][:], sq_a[t][:], sq_b[t][:], ALU.add)
+
+        def root(t):
+            nc.scalar.activation(ra[t][:], sq[t][:], ACT.Sqrt, bias=0.25)
+
+        def put_a(t):
+            nc.vector.tensor_copy(res[t][:].indirect(n4_l[:]), ra[t][:])
+            nc.sync.dma_start(out_rows[t], res[t][:])
+
+        nc.scalar.activation(h2[0][:, halves[0]], c0a[:], ACT.Copy)
+        nc.scalar.activation(h2[1][:, halves[0]], c1a[:], ACT.Copy)
+        nc.vector.tensor_copy(h2[0][:, halves[1]], c0b[:])
+        fetch_a(0)
+        nc.vector.tensor_copy(pb[0][:], h2[0][:].indirect(n5_l[:]))
+        put_b(0)
+        nc.scalar.activation(h2[1][:, halves[1]], c1b[:], ACT.Copy)
+        fetch_a(1)
+        fetch_b(1)
+        put_b(1)
+        squares(0)
+        squares(1)
+        root(0)
+        root(1)
+        put_a(0)
+        put_a(1)
+        for t, bank in ((2, c2), (3, c3)):
+            nc.scalar.activation(h2[t][:], bank[:], ACT.Copy)
+            fetch_a(t)
+            fetch_b(t)
+            put_b(t)
+        squares(2)
+        squares(3)
+        root(2)
+        root(3)
+        put_a(2)
+        put_a(3)

@@ -1,6 +1,7 @@
 from contextlib import ExitStack
 
 import concourse.mybir as mybir
+from concourse.masks import make_identity
 
 F32 = mybir.dt.float32
 BF16 = mybir.dt.bfloat16
@@ -29,8 +30,8 @@ def tile_picked_pqlayksetpolar_none_p_kernel(
         keep = ctx.enter_context(tc.tile_pool(name="keep", bufs=1))
         psum = ctx.enter_context(tc.psum_pool(name="psum", bufs=1))
 
-        def sb(name, shape, dtype):
-            return keep.tile(shape, dtype, name=name, align_bytes=64)
+        def sb(name, shape, dtype, tag=None):
+            return keep.tile(shape, dtype, name=name, tag=tag or name, align_bytes=64)
 
         def load_list(name, src):
             tile = keep.tile([P, src.shape[1]], U16, name=name)
@@ -45,6 +46,8 @@ def tile_picked_pqlayksetpolar_none_p_kernel(
         w_sraw = sb("w_sraw", [P, S], U8)
         gain = sb("gain", [P, PACK], F32)
 
+        nc.gpsimd.memset(x_stab[:].bitcast(I32), 0)
+        nc.scalar.dma_start(x_stab[0:P:8, :].bitcast(I32), x_scales[0].bitcast(I32))
         k1_l = load_list("k1_l", k1)
         nc.sync.dma_start(
             d_stab[:].bitcast(I32), d_scales[0].bitcast(I32).unsqueeze(1).broadcast_to([16, 8, TABLE // 4])
@@ -52,36 +55,41 @@ def tile_picked_pqlayksetpolar_none_p_kernel(
         offs_l = load_list("offs_l", offs)
         n2_l = load_list("n2_l", n2)
         n1_l = load_list("n1_l", n1)
+        n3_l = load_list("n3_l", n3)
         nc.sync.dma_start(d_tab[:].bitcast(I32), d_words[0].rearrange("p n t -> p (n t)").bitcast(I32))
         nc.sync.dma_start(x_tab[:].bitcast(I32), x_words[0].rearrange("p n t -> p (n t)").bitcast(I32))
-        n3_l = load_list("n3_l", n3)
         n4_l = load_list("n4_l", n4)
         n5_l = load_list("n5_l", n5)
-        nc.gpsimd.memset(x_stab[:].bitcast(I32), 0)
-        for q in range(4):
-            nc.gpsimd.dma_start(x_stab[32 * q : 32 * q + 4, :].bitcast(I32), x_scales[0, 4 * q : 4 * q + 4, :].bitcast(I32))
         nc.gpsimd.dma_start(gain[:], gn.rearrange("(p t) o -> p (t o)", t=PACK))
         nc.gpsimd.dma_start(w_raw[:].bitcast(I32), w1_words[0].bitcast(I32))
         nc.gpsimd.memset(w_sraw[:].bitcast(I32), 0)
         for q in range(4):
             nc.gpsimd.dma_start(w_sraw[32 * q : 32 * q + 4, :].bitcast(I32), w1_scales[0, 4 * q : 4 * q + 4, :].bitcast(I32))
 
+        ident = sb("ident", [P, P], F32)
+        make_identity(nc, ident[:])
+
         d_sg = sb("d_sg", [P, S], U8)
         nc.vector.tensor_copy(d_sg[:], d_stab[:].indirect(k1_l[:]))
-        d_s = sb("d_s", [P, S], U8)
+        spread = sb("spread", [P, 2 * S], U8)
+        planes = sb("planes", [P, 2 * S], U8)
+        nc.vector.memset(planes[:].bitcast(I32), 0)
+        d_s = planes[:, 0:S]
+        x_s = planes[:, S : 2 * S]
         nc.vector.tensor_copy(
-            d_s[:].rearrange("p (t m) -> p m t", t=PACK), d_sg[:].rearrange("p (m t) -> p m t", t=PACK)
+            spread[:, 0:S].rearrange("p (t m) -> p m t", t=PACK), d_sg[:].rearrange("p (m t) -> p m t", t=PACK)
         )
-        for j in range(1, 4):
-            nc.scalar.dma_start(d_s[j:P:32, :].bitcast(I32), d_s[8 * j : P : 32, :].bitcast(I32))
-        d_g = sb("d_g", [P, S], U32)
+        x_sg = sb("x_sg", [P, S], U8, "picked")
+        nc.vector.tensor_copy(x_sg[:], x_stab[:].indirect(offs_l[:]))
+        nc.vector.tensor_copy(spread[:, S : 2 * S].bitcast(I32), x_sg[:].bitcast(I32))
+        for q in range(4):
+            nc.sync.dma_start(planes[32 * q : 32 * q + 4, :].bitcast(I32), spread[32 * q : 32 * q + 32 : 8, :].bitcast(I32))
+        d_g = sb("d_g", [P, S], U32, "picked")
         nc.vector.tensor_copy(d_g[:], d_tab[:].indirect(k1_l[:]))
         d_w = sb("d_w", [P, S], U32)
         nc.vector.tensor_copy(
             d_w[:].rearrange("p (t m) -> p m t", t=PACK), d_g[:].rearrange("p (m t) -> p m t", t=PACK)
         )
-        x_s = sb("x_s", [P, S], U8)
-        nc.vector.tensor_copy(x_s[:], x_stab[:].indirect(offs_l[:]))
         x_w = sb("x_w", [P, S], U32)
         for u in range(2):
             nc.vector.tensor_copy(x_w[:, u * W : (u + 1) * W], x_tab[:].indirect(offs_l[:, 16 * u : 16 * (u + 1)]))
@@ -171,22 +179,22 @@ def tile_picked_pqlayksetpolar_none_p_kernel(
         def second(t, tag, cols):
             return product(tag, w_w[:, 2 * t * P : 2 * (t + 1) * P].bitcast(FP4X4), w_s[:, t * P : (t + 1) * P], z_w, z_s, cols)
 
-        c0a = second(0, "b6", halves[0])
-        c1a = second(1, "b7", halves[0])
-        c0b = second(0, "b0", halves[1])
-        c1b = second(1, "b1", halves[1])
-        c2 = second(2, "b4", whole)
-        c3 = second(3, "b5", whole)
+        low = [second(t, tag, halves[0]) for t, tag in ((0, "b6"), (1, "b7"), (2, "b0"))]
+        high = [second(0, "b1", halves[1])]
+        low.append(second(3, "b2", halves[0]))
+        high.extend(second(t, tag, halves[1]) for t, tag in ((1, "b3"), (2, "b4"), (3, "b5")))
+        turn_tags = ("b6", "b7", "b0", "b2")
+        sum_tags = ("b1", "b3", "b4", "b5")
 
         out_rows = out.rearrange("(p t) c -> t p c", t=PACK)
         h2 = [sb("h2_%d" % t, [P, S], F32) for t in range(PACK)]
         half_a = [sb("half_a%d" % t, [P, W], F32) for t in range(PACK)]
         pb = [sb("pb%d" % t, [P, W], F32) for t in range(PACK)]
-        sq_a = [sb("sq_a%d" % t, [P, W], F32) for t in range(PACK)]
-        sq_b = [sb("sq_b%d" % t, [P, W], F32) for t in range(PACK)]
-        sq = [sb("sq%d" % t, [P, W], F32) for t in range(PACK)]
+        sq = [sb("sq%d" % t, [P, S], F32) for t in range(PACK)]
         ra = [sb("ra%d" % t, [P, W], F32) for t in range(PACK)]
         res = [sb("res%d" % t, [P, S], F32) for t in range(PACK)]
+        turned = []
+        sums = []
 
         def fetch_a(t):
             nc.scalar.activation(half_a[t][:], h2[t][:].indirect(n4_l[:]), ACT.Copy, scale=-0.5)
@@ -196,43 +204,48 @@ def tile_picked_pqlayksetpolar_none_p_kernel(
 
         def put_b(t):
             nc.vector.tensor_tensor(res[t][:].indirect(n5_l[:]), pb[t][:], half_a[t][:], ALU.add)
+            bank = psum.tile([P, S], F32, name="bank", tag=turn_tags[t])
+            for i, src in enumerate((half_a[t], pb[t])):
+                for b in range(2):
+                    nc.tensor.transpose(bank[:, i * W + b * P : i * W + (b + 1) * P], src[:, b * P : (b + 1) * P], ident[:])
+            turned.append(bank)
 
         def squares(t):
-            nc.scalar.activation(sq_a[t][:], half_a[t][:], ACT.Square, scale=2.0)
-            nc.scalar.activation(sq_b[t][:], pb[t][:], ACT.Square)
-            nc.vector.tensor_tensor(sq[t][:], sq_a[t][:], sq_b[t][:], ALU.add)
+            nc.scalar.activation(sq[t][:, halves[0]], turned[t][:, halves[0]], ACT.Square, scale=2.0)
+            nc.scalar.activation(sq[t][:, halves[1]], turned[t][:, halves[1]], ACT.Square)
+            bank = psum.tile([P, W], F32, name="bank", tag=sum_tags[t])
+            for b in range(2):
+                for i in range(2):
+                    nc.tensor.matmul(
+                        bank[:, b * P : (b + 1) * P],
+                        lhsT=sq[t][:, i * W + b * P : i * W + (b + 1) * P],
+                        rhs=ident[:],
+                        is_transpose=True,
+                        start=(i == 0),
+                        stop=(i == 1),
+                    )
+            sums.append(bank)
 
         def root(t):
-            nc.scalar.activation(ra[t][:], sq[t][:], ACT.Sqrt, bias=0.25)
-
-        def put_a(t):
+            nc.scalar.activation(ra[t][:], sums[t][:], ACT.Sqrt, bias=0.25)
             nc.vector.tensor_copy(res[t][:].indirect(n4_l[:]), ra[t][:])
             nc.sync.dma_start(out_rows[t], res[t][:])
 
-        nc.scalar.activation(h2[0][:, halves[0]], c0a[:], ACT.Copy)
-        nc.scalar.activation(h2[1][:, halves[0]], c1a[:], ACT.Copy)
-        nc.vector.tensor_copy(h2[0][:, halves[1]], c0b[:])
+        for t in range(PACK - 1):
+            nc.scalar.activation(h2[t][:, halves[0]], low[t][:], ACT.Copy)
+        nc.vector.tensor_copy(h2[0][:, halves[1]], high[0][:])
         fetch_a(0)
         nc.vector.tensor_copy(pb[0][:], h2[0][:].indirect(n5_l[:]))
         put_b(0)
-        nc.scalar.activation(h2[1][:, halves[1]], c1b[:], ACT.Copy)
-        fetch_a(1)
-        fetch_b(1)
-        put_b(1)
-        squares(0)
-        squares(1)
-        root(0)
-        root(1)
-        put_a(0)
-        put_a(1)
-        for t, bank in ((2, c2), (3, c3)):
-            nc.scalar.activation(h2[t][:], bank[:], ACT.Copy)
+        for t in range(1, PACK):
+            if t == PACK - 1:
+                nc.scalar.activation(h2[t][:, halves[0]], low[t][:], ACT.Copy)
+            nc.scalar.activation(h2[t][:, halves[1]], high[t][:], ACT.Copy)
             fetch_a(t)
             fetch_b(t)
             put_b(t)
-        squares(2)
-        squares(3)
-        root(2)
-        root(3)
-        put_a(2)
-        put_a(3)
+        squares(0)
+        for t in range(1, PACK):
+            squares(t)
+            root(t - 1)
+        root(PACK - 1)

@@ -48,6 +48,10 @@ def tile_picked_pqlayksetpolar_none_p_kernel(
 
         nc.gpsimd.memset(x_stab[:].bitcast(I32), 0)
         nc.scalar.dma_start(x_stab[0:P:8, :].bitcast(I32), x_scales[0].bitcast(I32))
+        warm = sb("warm", [P, 1], F32)
+        nc.gpsimd.memset(warm[:], 1.0)
+        warm_out = sb("warm_out", [P, 1], F32)
+        nc.scalar.activation(warm_out[:], warm[:], ACT.Sqrt)
         k1_l = load_list("k1_l", k1)
         nc.sync.dma_start(
             d_stab[:].bitcast(I32), d_scales[0].bitcast(I32).unsqueeze(1).broadcast_to([16, 8, TABLE // 4])

@@ -44,6 +44,7 @@ def tile_picked_pqlayksetpolar_none_p_kernel(
         x_stab = sb("x_stab", [P, TABLE], U8)
         w_raw = sb("w_raw", [P, 2 * S], U8)
         w_sraw = sb("w_sraw", [P, S], U8)
+        gain_raw = sb("gain_raw", [P, PACK], F32)
         gain = sb("gain", [P, PACK], F32)
 
         nc.gpsimd.memset(x_stab[:].bitcast(I32), 0)
@@ -64,17 +65,18 @@ def tile_picked_pqlayksetpolar_none_p_kernel(
         nc.sync.dma_start(x_tab[:].bitcast(I32), x_words[0].rearrange("p n t -> p (n t)").bitcast(I32))
         n4_l = load_list("n4_l", n4)
         n5_l = load_list("n5_l", n5)
-        nc.gpsimd.dma_start(gain[:], gn.rearrange("(p t) o -> p (t o)", t=PACK))
+        ident = sb("ident", [P, P], F32)
+        make_identity(nc, ident[:])
+        nc.gpsimd.dma_start(gain_raw[:], gn.rearrange("(p t) o -> p (t o)", t=PACK))
         nc.gpsimd.dma_start(w_raw[:].bitcast(I32), w1_words[0].bitcast(I32))
-        nc.gpsimd.memset(w_sraw[:].bitcast(I32), 0)
+        nc.vector.memset(w_sraw[:].bitcast(I32), 0)
         for q in range(4):
             nc.gpsimd.dma_start(w_sraw[32 * q : 32 * q + 4, :].bitcast(I32), w1_scales[0, 4 * q : 4 * q + 4, :].bitcast(I32))
 
-        ident = sb("ident", [P, P], F32)
-        make_identity(nc, ident[:])
-
         d_sg = sb("d_sg", [P, S], U8)
         nc.vector.tensor_copy(d_sg[:], d_stab[:].indirect(k1_l[:]))
+        x_sg = sb("x_sg", [P, S], U8, "picked")
+        nc.vector.tensor_copy(x_sg[:], x_stab[:].indirect(offs_l[:]))
         spread = sb("spread", [P, 2 * S], U8)
         planes = sb("planes", [P, 2 * S], U8)
         nc.vector.memset(planes[:].bitcast(I32), 0)
@@ -83,8 +85,6 @@ def tile_picked_pqlayksetpolar_none_p_kernel(
         nc.vector.tensor_copy(
             spread[:, 0:S].rearrange("p (t m) -> p m t", t=PACK), d_sg[:].rearrange("p (m t) -> p m t", t=PACK)
         )
-        x_sg = sb("x_sg", [P, S], U8, "picked")
-        nc.vector.tensor_copy(x_sg[:], x_stab[:].indirect(offs_l[:]))
         nc.vector.tensor_copy(spread[:, S : 2 * S].bitcast(I32), x_sg[:].bitcast(I32))
         for q in range(4):
             nc.sync.dma_start(planes[32 * q : 32 * q + 4, :].bitcast(I32), spread[32 * q : 32 * q + 32 : 8, :].bitcast(I32))
@@ -98,14 +98,16 @@ def tile_picked_pqlayksetpolar_none_p_kernel(
         for u in range(2):
             nc.vector.tensor_copy(x_w[:, u * W : (u + 1) * W], x_tab[:].indirect(offs_l[:, 16 * u : 16 * (u + 1)]))
 
-        w_s = sb("w_s", [P, S], U8)
-        nc.gpsimd.tensor_copy(
-            w_s[:].rearrange("p (t m) -> p t m", t=PACK), w_sraw[:].rearrange("p (m t) -> p t m", t=PACK)
-        )
+        nc.scalar.activation(gain[:], gain_raw[:], ACT.Copy, scale=0.0625)
         w_w = sb("w_w", [P, 2 * S], U8)
         nc.scalar.copy(
-            w_w[:].bitcast(U16).rearrange("p (t m) -> p m t", t=PACK),
-            w_raw[:].bitcast(U16).rearrange("p (m t) -> p m t", t=PACK),
+            w_w[:].bitcast(U32).rearrange("p (t m e) -> p t m e", t=PACK, e=2),
+            w_raw[:].bitcast(U32).rearrange("p (m t e) -> p t m e", t=PACK, e=2),
+        )
+        w_s = sb("w_s", [P, S], U8)
+        nc.scalar.copy(
+            w_s[:].bitcast(U32).rearrange("p (t m) -> p t m", t=PACK),
+            w_sraw[:].bitcast(U32).rearrange("p (m t) -> p t m", t=PACK),
         )
 
         halves = [slice(0, W), slice(W, S)]
@@ -132,38 +134,45 @@ def tile_picked_pqlayksetpolar_none_p_kernel(
             own = slice(t * P, (t + 1) * P)
             return product(tag, d_w[:, own].bitcast(FP8X4), d_s[:, own], x_w, x_s, cols)
 
-        whole = slice(0, S)
-        b0a = first(0, "b0", halves[0])
-        b1a = first(1, "b1", halves[0])
-        b0b = first(0, "b2", halves[1])
-        b1b = first(1, "b3", halves[1])
-        b2 = first(2, "b4", whole)
-        b3 = first(3, "b5", whole)
+        low = [first(t, "b%d" % t, halves[0]) for t in range(2)]
+        high = [first(t, "b%d" % (2 + t), halves[1]) for t in range(2)]
+        full = [first(t, "b%d" % (2 + t), slice(0, S)) for t in range(2, PACK)]
 
-        nc.scalar.activation(ds[0][:, halves[0]], b0a[:], ACT.Copy, scale=gain[:, 0:1])
-        nc.scalar.activation(ds[1][:, halves[0]], b1a[:], ACT.Copy, scale=gain[:, 1:2])
-        nc.vector.tensor_scalar(ds[0][:, halves[1]], b0b[:], gain[:, 0:1], None, ALU.mult)
-        nc.scalar.activation(pa[0][:, 0:128], ds[0][:].indirect(n2_l[:, 0:8]), ACT.Copy)
-        nc.vector.tensor_copy(pa[0][:, 128:256], ds[0][:].indirect(n2_l[:, 8:16]))
-        nc.vector.tensor_copy(ds[0][:].indirect(n1_l[:]), pa[0][:])
-        nc.scalar.activation(ds[1][:, halves[1]], b1b[:], ACT.Copy, scale=gain[:, 1:2])
-        for t, bank in ((1, None), (2, b2), (3, b3)):
-            if bank is not None:
-                nc.scalar.activation(ds[t][:], bank[:], ACT.Copy, scale=gain[:, t : t + 1])
+        def empty(t, cols, bank):
+            nc.scalar.activation(ds[t][:, cols], bank[:], ACT.Copy, scale=gain[:, t : t + 1])
+
+        def patch(t):
             nc.scalar.activation(pa[t][:], ds[t][:].indirect(n2_l[:]), ACT.Copy)
             nc.vector.tensor_copy(ds[t][:].indirect(n1_l[:]), pa[t][:])
 
+        empty(0, halves[0], low[0])
+        empty(1, halves[0], low[1])
+        nc.vector.tensor_scalar(ds[0][:, halves[1]], high[0][:], gain[:, 0:1], None, ALU.mult)
+        empty(1, halves[1], high[1])
+        nc.scalar.activation(pa[0][:, 0:128], ds[0][:].indirect(n2_l[:, 0:8]), ACT.Copy)
+        nc.vector.tensor_copy(pa[0][:, 128:256], ds[0][:].indirect(n2_l[:, 8:16]))
+        nc.vector.tensor_copy(ds[0][:].indirect(n1_l[:]), pa[0][:])
+        patch(1)
+        empty(2, slice(0, S), full[0])
+        empty(3, slice(0, S), full[1])
+        patch(2)
+        patch(3)
+
+        def fetch_far(t, u):
+            window = ds[t][:].indirect(n3_l[:, 16 * u : 16 * (u + 1)])
+            if (t, u) == (PACK - 1, 1):
+                nc.vector.tensor_scalar(far[t][:, halves[u]], window, -0.5, 0.0, ALU.mult, ALU.add)
+            else:
+                nc.scalar.activation(far[t][:, halves[u]], window, ACT.Copy, scale=-0.5)
+
         for t in range(PACK):
             for u in (1, 0):
-                nc.scalar.activation(
-                    far[t][:, halves[u]], ds[t][:].indirect(n3_l[:, 16 * u : 16 * (u + 1)]), ACT.Copy, scale=-0.03125
-                )
-        for t in range(PACK - 1):
-            nc.vector.scalar_tensor_tensor(z_planes[:, t, :], ds[t][:], 0.0625, far[t][:], ALU.mult, ALU.add)
+                fetch_far(t, u)
+        for t in range(2):
+            nc.gpsimd.tensor_tensor(z_planes[:, t, :], ds[t][:], far[t][:], ALU.add)
         for u in (1, 0):
-            nc.vector.scalar_tensor_tensor(
-                z_planes[:, 3, halves[u]], ds[3][:, halves[u]], 0.0625, far[3][:, halves[u]], ALU.mult, ALU.add
-            )
+            for t in range(2, PACK):
+                nc.vector.tensor_tensor(z_planes[:, t, halves[u]], ds[t][:, halves[u]], far[t][:, halves[u]], ALU.add)
 
         z_k = [sb("z_k%d" % u, [P, W, PACK], BF16) for u in range(2)]
         z_w = sb("z_w", [P, S], U32)
@@ -173,7 +182,7 @@ def tile_picked_pqlayksetpolar_none_p_kernel(
                 z_k[u][:].rearrange("p (c i) t -> p c t i", i=4),
                 z_planes[:, :, halves[u]].rearrange("p t (c i) -> p c t i", i=4),
             )
-        for u in range(2):
+        for u in (1, 0):
             nc.vector.quantize_mx(
                 out=z_w[:, halves[u]].bitcast(FP8X4),
                 scales=z_s[:, halves[u]],
@@ -183,14 +192,14 @@ def tile_picked_pqlayksetpolar_none_p_kernel(
         def second(t, tag, cols):
             return product(tag, w_w[:, 2 * t * P : 2 * (t + 1) * P].bitcast(FP4X4), w_s[:, t * P : (t + 1) * P], z_w, z_s, cols)
 
-        low = [second(t, tag, halves[0]) for t, tag in ((0, "b6"), (1, "b7"), (2, "b0"))]
-        high = [second(0, "b1", halves[1])]
-        low.append(second(3, "b2", halves[0]))
-        high.extend(second(t, tag, halves[1]) for t, tag in ((1, "b3"), (2, "b4"), (3, "b5")))
+        early = [second(t, tag, halves[1]) for t, tag in ((0, "b6"), (1, "b7"), (2, "b0"))]
+        late = [second(0, "b1", halves[0])]
+        early.append(second(3, "b2", halves[1]))
+        late.extend(second(t, tag, halves[0]) for t, tag in ((1, "b3"), (2, "b4"), (3, "b5")))
         turn_tags = ("b6", "b7", "b0", "b2")
         sum_tags = ("b1", "b3", "b4", "b5")
 
-        out_rows = out.rearrange("(p t) c -> t p c", t=PACK)
+        out_rows = out.rearrange("(m t e) c -> t m e c", t=PACK, e=4)
         h2 = [sb("h2_%d" % t, [P, S], F32) for t in range(PACK)]
         half_a = [sb("half_a%d" % t, [P, W], F32) for t in range(PACK)]
         pb = [sb("pb%d" % t, [P, W], F32) for t in range(PACK)]
@@ -236,15 +245,15 @@ def tile_picked_pqlayksetpolar_none_p_kernel(
             nc.sync.dma_start(out_rows[t], res[t][:])
 
         for t in range(PACK - 1):
-            nc.scalar.activation(h2[t][:, halves[0]], low[t][:], ACT.Copy)
-        nc.vector.tensor_copy(h2[0][:, halves[1]], high[0][:])
+            nc.scalar.activation(h2[t][:, halves[1]], early[t][:], ACT.Copy)
+        nc.vector.tensor_copy(h2[0][:, halves[0]], late[0][:])
         fetch_a(0)
         nc.vector.tensor_copy(pb[0][:], h2[0][:].indirect(n5_l[:]))
         put_b(0)
         for t in range(1, PACK):
             if t == PACK - 1:
-                nc.scalar.activation(h2[t][:, halves[0]], low[t][:], ACT.Copy)
-            nc.scalar.activation(h2[t][:, halves[1]], high[t][:], ACT.Copy)
+                nc.scalar.activation(h2[t][:, halves[1]], early[t][:], ACT.Copy)
+            nc.scalar.activation(h2[t][:, halves[0]], late[t][:], ACT.Copy)
             fetch_a(t)
             fetch_b(t)
             put_b(t)

from contextlib import ExitStack

import concourse.mybir as mybir
from concourse.masks import make_identity

F32 = mybir.dt.float32
BF16 = mybir.dt.bfloat16
I32 = mybir.dt.int32
U32 = mybir.dt.uint32
U16 = mybir.dt.uint16
U8 = mybir.dt.uint8
FP8X4 = mybir.dt.float8_e4m3fn_x4
FP4X4 = mybir.dt.float4_e2m1fn_x4
ACT = mybir.ActivationFunctionType
ALU = mybir.AluOpType

P = 128
PACK = 4
TABLE = 2048
S = 512
W = 256
FLOPS = 2 * 2 * 512 * 512 * 512


def tile_picked_pqlayksetpolar_none_p_kernel(
    tc, x_words, x_scales, d_words, d_scales, gn, w1_words, w1_scales, offs, k1, n1, n2, n3, n4, n5, out
):
    nc = tc.nc
    with ExitStack() as ctx:
        keep = ctx.enter_context(tc.tile_pool(name="keep", bufs=1))
        psum = ctx.enter_context(tc.psum_pool(name="psum", bufs=1))

        def sb(name, shape, dtype, tag=None):
            return keep.tile(shape, dtype, name=name, tag=tag or name, align_bytes=64)

        def load_list(name, src):
            tile = keep.tile([P, src.shape[1]], U16, name=name)
            nc.sync.dma_start(tile[:], src)
            return tile

        d_tab = sb("d_tab", [P, TABLE], U32)
        x_tab = sb("x_tab", [P, TABLE], U32)
        d_stab = sb("d_stab", [P, TABLE], U8)
        x_stab = sb("x_stab", [P, TABLE], U8)
        w_raw = sb("w_raw", [P, 2 * S], U8)
        w_sraw = sb("w_sraw", [P, S], U8)
        gain_raw = sb("gain_raw", [P, PACK], F32)
        gain = sb("gain", [P, PACK], F32)

        nc.gpsimd.memset(x_stab[:].bitcast(I32), 0)
        nc.scalar.dma_start(x_stab[0:P:8, :].bitcast(I32), x_scales[0].bitcast(I32))
        warm = sb("warm", [P, 1], F32)
        nc.gpsimd.memset(warm[:], 1.0)
        warm_out = sb("warm_out", [P, 1], F32)
        nc.scalar.activation(warm_out[:], warm[:], ACT.Sqrt)
        k1_l = load_list("k1_l", k1)
        nc.sync.dma_start(
            d_stab[:].bitcast(I32), d_scales[0].bitcast(I32).unsqueeze(1).broadcast_to([16, 8, TABLE // 4])
        )
        offs_l = load_list("offs_l", offs)
        n2_l = load_list("n2_l", n2)
        n1_l = load_list("n1_l", n1)
        n3_l = load_list("n3_l", n3)
        nc.sync.dma_start(d_tab[:].bitcast(I32), d_words[0].rearrange("p n t -> p (n t)").bitcast(I32))
        nc.sync.dma_start(x_tab[:].bitcast(I32), x_words[0].rearrange("p n t -> p (n t)").bitcast(I32))
        n4_l = load_list("n4_l", n4)
        n5_l = load_list("n5_l", n5)
        ident = sb("ident", [P, P], F32)
        make_identity(nc, ident[:])
        nc.gpsimd.dma_start(gain_raw[:], gn.rearrange("(p t) o -> p (t o)", t=PACK))
        nc.gpsimd.dma_start(w_raw[:].bitcast(I32), w1_words[0].bitcast(I32))
        nc.vector.memset(w_sraw[:].bitcast(I32), 0)
        for q in range(4):
            nc.gpsimd.dma_start(w_sraw[32 * q : 32 * q + 4, :].bitcast(I32), w1_scales[0, 4 * q : 4 * q + 4, :].bitcast(I32))

        d_sg = sb("d_sg", [P, S], U8)
        nc.vector.tensor_copy(d_sg[:], d_stab[:].indirect(k1_l[:]))
        x_sg = sb("x_sg", [P, S], U8, "picked")
        nc.vector.tensor_copy(x_sg[:], x_stab[:].indirect(offs_l[:]))
        spread = sb("spread", [P, 2 * S], U8)
        planes = sb("planes", [P, 2 * S], U8)
        nc.vector.memset(planes[:].bitcast(I32), 0)
        d_s = planes[:, 0:S]
        x_s = planes[:, S : 2 * S]
        nc.vector.tensor_copy(
            spread[:, 0:S].rearrange("p (t m) -> p m t", t=PACK), d_sg[:].rearrange("p (m t) -> p m t", t=PACK)
        )
        nc.vector.tensor_copy(spread[:, S : 2 * S].bitcast(I32), x_sg[:].bitcast(I32))
        for q in range(4):
            nc.sync.dma_start(planes[32 * q : 32 * q + 4, :].bitcast(I32), spread[32 * q : 32 * q + 32 : 8, :].bitcast(I32))
        d_g = sb("d_g", [P, S], U32, "picked")
        nc.vector.tensor_copy(d_g[:], d_tab[:].indirect(k1_l[:]))
        d_w = sb("d_w", [P, S], U32)
        nc.vector.tensor_copy(
            d_w[:].rearrange("p (t m) -> p m t", t=PACK), d_g[:].rearrange("p (m t) -> p m t", t=PACK)
        )
        x_w = sb("x_w", [P, S], U32)
        for u in range(2):
            nc.vector.tensor_copy(x_w[:, u * W : (u + 1) * W], x_tab[:].indirect(offs_l[:, 16 * u : 16 * (u + 1)]))

        nc.scalar.activation(gain[:], gain_raw[:], ACT.Copy, scale=0.0625)
        w_w = sb("w_w", [P, 2 * S], U8)
        nc.scalar.copy(
            w_w[:].bitcast(U32).rearrange("p (t m e) -> p t m e", t=PACK, e=2),
            w_raw[:].bitcast(U32).rearrange("p (m t e) -> p t m e", t=PACK, e=2),
        )
        w_s = sb("w_s", [P, S], U8)
        nc.scalar.copy(
            w_s[:].bitcast(U32).rearrange("p (t m) -> p t m", t=PACK),
            w_sraw[:].bitcast(U32).rearrange("p (m t) -> p t m", t=PACK),
        )

        halves = [slice(0, W), slice(W, S)]

        def product(tag, lhsT, lhsT_scale, rhs_w, rhs_s, cols):
            bank = psum.tile([P, cols.stop - cols.start], F32, name="bank", tag=tag)
            nc.tensor.matmul_mx(
                out=bank[:],
                lhsT=lhsT,
                lhsT_scale=lhsT_scale,
                rhs=rhs_w[:, cols].bitcast(FP8X4),
                rhs_scale=rhs_s[:, cols],
                start=True,
                stop=True,
            )
            return bank

        ds = [sb("ds%d" % t, [P, S], F32) for t in range(PACK)]
        pa = [sb("pa%d" % t, [P, W], F32) for t in range(PACK)]
        far = [sb("far%d" % t, [P, S], F32) for t in range(PACK)]
        z_planes = sb("z_planes", [P, PACK, S], BF16)

        def first(t, tag, cols):
            own = slice(t * P, (t + 1) * P)
            return product(tag, d_w[:, own].bitcast(FP8X4), d_s[:, own], x_w, x_s, cols)

        low = [first(t, "b%d" % t, halves[0]) for t in range(2)]
        high = [first(t, "b%d" % (2 + t), halves[1]) for t in range(2)]
        full = [first(t, "b%d" % (2 + t), slice(0, S)) for t in range(2, PACK)]

        def empty(t, cols, bank):
            nc.scalar.activation(ds[t][:, cols], bank[:], ACT.Copy, scale=gain[:, t : t + 1])

        def patch(t):
            nc.scalar.activation(pa[t][:], ds[t][:].indirect(n2_l[:]), ACT.Copy)
            nc.vector.tensor_copy(ds[t][:].indirect(n1_l[:]), pa[t][:])

        empty(0, halves[0], low[0])
        empty(1, halves[0], low[1])
        nc.vector.tensor_scalar(ds[0][:, halves[1]], high[0][:], gain[:, 0:1], None, ALU.mult)
        empty(1, halves[1], high[1])
        nc.scalar.activation(pa[0][:, 0:128], ds[0][:].indirect(n2_l[:, 0:8]), ACT.Copy)
        nc.vector.tensor_copy(pa[0][:, 128:256], ds[0][:].indirect(n2_l[:, 8:16]))
        nc.vector.tensor_copy(ds[0][:].indirect(n1_l[:]), pa[0][:])
        patch(1)
        empty(2, slice(0, S), full[0])
        empty(3, slice(0, S), full[1])
        patch(2)
        patch(3)

        def fetch_far(t, u):
            window = ds[t][:].indirect(n3_l[:, 16 * u : 16 * (u + 1)])
            if (t, u) == (PACK - 1, 1):
                nc.vector.tensor_scalar(far[t][:, halves[u]], window, -0.5, 0.0, ALU.mult, ALU.add)
            else:
                nc.scalar.activation(far[t][:, halves[u]], window, ACT.Copy, scale=-0.5)

        for t in range(PACK):
            for u in (1, 0):
                fetch_far(t, u)
        for t in range(2):
            nc.gpsimd.tensor_tensor(z_planes[:, t, :], ds[t][:], far[t][:], ALU.add)
        for u in (1, 0):
            for t in range(2, PACK):
                nc.vector.tensor_tensor(z_planes[:, t, halves[u]], ds[t][:, halves[u]], far[t][:, halves[u]], ALU.add)

        z_k = [sb("z_k%d" % u, [P, W, PACK], BF16) for u in range(2)]
        z_w = sb("z_w", [P, S], U32)
        z_s = sb("z_s", [P, S], U8)
        for u, copy in ((1, nc.scalar.copy), (0, nc.vector.tensor_copy)):
            copy(
                z_k[u][:].rearrange("p (c i) t -> p c t i", i=4),
                z_planes[:, :, halves[u]].rearrange("p t (c i) -> p c t i", i=4),
            )
        for u in (1, 0):
            nc.vector.quantize_mx(
                out=z_w[:, halves[u]].bitcast(FP8X4),
                scales=z_s[:, halves[u]],
                in_=z_k[u][:].rearrange("p c t -> p (c t)"),
            )

        def second(t, tag, cols):
            return product(tag, w_w[:, 2 * t * P : 2 * (t + 1) * P].bitcast(FP4X4), w_s[:, t * P : (t + 1) * P], z_w, z_s, cols)

        early = [second(t, tag, halves[1]) for t, tag in ((0, "b6"), (1, "b7"), (2, "b0"))]
        late = [second(0, "b1", halves[0])]
        early.append(second(3, "b2", halves[1]))
        late.extend(second(t, tag, halves[0]) for t, tag in ((1, "b3"), (2, "b4"), (3, "b5")))
        turn_tags = ("b6", "b7", "b0", "b2")
        sum_tags = ("b1", "b3", "b4", "b5")

        out_rows = out.rearrange("(m t e) c -> t m e c", t=PACK, e=4)
        h2 = [sb("h2_%d" % t, [P, S], F32) for t in range(PACK)]
        half_a = [sb("half_a%d" % t, [P, W], F32) for t in range(PACK)]
        pb = [sb("pb%d" % t, [P, W], F32) for t in range(PACK)]
        sq = [sb("sq%d" % t, [P, S], F32) for t in range(PACK)]
        ra = [sb("ra%d" % t, [P, W], F32) for t in range(PACK)]
        res = [sb("res%d" % t, [P, S], F32) for t in range(PACK)]
        turned = []
        sums = []

        def fetch_a(t):
            nc.scalar.activation(half_a[t][:], h2[t][:].indirect(n4_l[:]), ACT.Copy, scale=-0.5)

        def fetch_b(t):
            nc.scalar.activation(pb[t][:], h2[t][:].indirect(n5_l[:]), ACT.Copy)

        def put_b(t):
            nc.vector.tensor_tensor(res[t][:].indirect(n5_l[:]), pb[t][:], half_a[t][:], ALU.add)
            bank = psum.tile([P, S], F32, name="bank", tag=turn_tags[t])
            for i, src in enumerate((half_a[t], pb[t])):
                for b in range(2):
                    nc.tensor.transpose(bank[:, i * W + b * P : i * W + (b + 1) * P], src[:, b * P : (b + 1) * P], ident[:])
            turned.append(bank)

        def squares(t):
            nc.scalar.activation(sq[t][:, halves[0]], turned[t][:, halves[0]], ACT.Square, scale=2.0)
            nc.scalar.activation(sq[t][:, halves[1]], turned[t][:, halves[1]], ACT.Square)
            bank = psum.tile([P, W], F32, name="bank", tag=sum_tags[t])
            for b in range(2):
                for i in range(2):
                    nc.tensor.matmul(
                        bank[:, b * P : (b + 1) * P],
                        lhsT=sq[t][:, i * W + b * P : i * W + (b + 1) * P],
                        rhs=ident[:],
                        is_transpose=True,
                        start=(i == 0),
                        stop=(i == 1),
                    )
            sums.append(bank)

        def root(t):
            nc.scalar.activation(ra[t][:], sums[t][:], ACT.Sqrt, bias=0.25)
            nc.vector.tensor_copy(res[t][:].indirect(n4_l[:]), ra[t][:])
            nc.sync.dma_start(out_rows[t], res[t][:])

        for t in range(PACK - 1):
            nc.scalar.activation(h2[t][:, halves[1]], early[t][:], ACT.Copy)
        nc.vector.tensor_copy(h2[0][:, halves[0]], late[0][:])
        fetch_a(0)
        nc.vector.tensor_copy(pb[0][:], h2[0][:].indirect(n5_l[:]))
        put_b(0)
        for t in range(1, PACK):
            if t == PACK - 1:
                nc.scalar.activation(h2[t][:, halves[1]], early[t][:], ACT.Copy)
            nc.scalar.activation(h2[t][:, halves[0]], late[t][:], ACT.Copy)
            fetch_a(t)
            fetch_b(t)
            put_b(t)
        squares(0)
        for t in range(1, PACK):
            squares(t)
            root(t - 1)
        root(PACK - 1)
